import numpy as np, ml_dtypes
CORES = [51,54,179,182]
N = 4
import mx_ref
NC, G = 128, 2
C, C2 = np.float32(0.031), np.float32(0.0155)
BF = ml_dtypes.bfloat16
def cut(t, i, w=512):
    return t[:, w * i:w * i + w]
def tile(rs):
    return np.stack(rs, axis=2).reshape(128, -1).astype(BF)
def layer(w, X):
    out = []
    for i in range(G):
        for t in range(len(X)):
            p = mx_ref.matmul(mx_ref.quantize(cut(w, len(X) * i + t)), X[t])
            z = p if t == 0 else z + p
        out.append(z)
    return out
def act(Z):
    return [np.maximum(s * z, 0) * C for z in Z for s in (1, -1)]
def act2(Z):
    return [np.maximum(s * z, 0) * C2 for z in Z for s in (1, -1)]
def setup_inputs(rng):
    def f(*shape):
        return mx_ref.flush((rng.standard_normal(shape, dtype=np.float32) * np.exp2(rng.integers(-2, 3, shape[:-1] + (1,)))).astype(BF))
    return {"x": f(N, 128, 4 * NC), "w1": f(N, 128, G * 512), "w2": f(N, 128, G * 512), "w3": f(N, 128, G * 512)}
def setup_inputs_blocks(rng):
    d = setup_inputs(rng)
    for k in ("x", "w1", "w2", "w3"): d[k] = mx_ref.spread(d[k], rng, 2)
    return d
def setup_inputs_wide(rng):
    d = setup_inputs(rng)
    for k in ("x", "w1", "w2", "w3"): d[k] = mx_ref.flush((d[k].astype(np.float32) * np.exp2(rng.integers(-4, 5, (N, 1, 1))).astype(np.float32)).astype(BF))
    return d
def reference(x, w1, w2, w3, own=None):
    X = [mx_ref.quantize(x[j]) for j in range(N)]
    t = np.stack([np.stack([tile(act(layer(w1[r], [X[c]]))) for c in range(N)]) for r in range(N)])
    uset = t if own is None else own["t"]
    h = np.zeros((N, 128, 4 * NC), BF)
    for c in range(N):
        for r in range(N):
            P = layer(w2[r], [mx_ref.quantize(uset[r][c])])
            Z = P if r == 0 else [z + p for z, p in zip(Z, P)]
        h[c] = tile(act2(Z))
    use = h if own is None else own["h"]
    H = [mx_ref.quantize(use[j]) for j in range(N)]
    y = np.zeros((N, 128, N * G * NC), np.float32)
    for r in range(N):
        for j in range(N):
            Z = layer(w3[r], [H[j]])
            for i in range(G):
                y[r][:, NC * (G * j + i):NC * (G * j + i) + NC] = Z[i]
    return {"t": t, "h": h, "y": y}

@@ -1,0 +1,225 @@
+from concourse.bass import DstId, RemoteDMATransfer
+from concourse.mybir import dt, AluOpType, ActivationFunctionType
+
+N = 4
+NC = 128
+C1, C2 = 0.031, 0.0155
+U8 = dt.uint8
+
+SCRATCH = {
+    "xb": ("sbuf", [128, 512], "bfloat16"),
+    "w1b": ("sbuf", [128, 1024], "bfloat16"),
+    "w2b": ("sbuf", [128, 1024], "bfloat16"),
+    "w3b": ("sbuf", [128, 1024], "bfloat16"),
+    "xq": ("sbuf", [128, N * NC], "float8_e4m3fn_x4"),
+    "xs": ("sbuf", [128, N * NC], "uint8"),
+    "w1q": ("sbuf", [128, 256], "float8_e4m3fn_x4"),
+    "w1s": ("sbuf", [128, 256], "uint8"),
+    "w2q": ("sbuf", [128, 256], "float8_e4m3fn_x4"),
+    "w2s": ("sbuf", [128, 256], "uint8"),
+    "w3q": ("sbuf", [128, 256], "float8_e4m3fn_x4"),
+    "w3s": ("sbuf", [128, 256], "uint8"),
+    "tq": ("sbuf", [128, N * NC], "float8_e4m3fn_x4"),
+    "ts": ("sbuf", [128, N * NC], "uint8"),
+    "hq": ("sbuf", [128, N * NC], "float8_e4m3fn_x4"),
+    "hs": ("sbuf", [128, N * NC], "uint8"),
+    "tt": ("sbuf", [128, N * 512], "bfloat16"),
+    "ht": ("sbuf", [128, 512], "bfloat16"),
+    "acc0": ("sbuf", [128, 256], "float32"),
+    "acc1": ("sbuf", [128, 256], "float32"),
+    "acc2": ("sbuf", [128, 256], "float32"),
+    "yt": ("sbuf", [128, N * 256], "float32"),
+}
+for _c in range(N):
+    SCRATCH["po%d" % _c] = ("sbuf", [128, 256], "float32")
+    SCRATCH["pi%d" % _c] = ("sbuf", [128, 256], "float32")
+for _k in range(8):
+    SCRATCH["ps%d" % _k] = ("psum", [128, 512], "float32")
+
+SEMAPHORES = ["lx", "l1", "l2", "l3", "qx", "q1", "q2", "q3", "ad0", "ad1", "ad2", "ad3", "ha", "hq",
+              "xlc", "xlm", "plc", "plm", "hl", "st"]
+for _c in range(N):
+    for _s in ("xr", "pr", "hr", "z0_", "z1_", "ta", "tq", "p0_", "p1_", "pc", "y0_", "y1_", "yc"):
+        SEMAPHORES.append("%s%d" % (_s, _c))
+
+
+def rank_program(g, core, T, topo):
+    r = T.rank_of(core)
+    if r is None:
+        return
+    cores = T.cores
+    S = T.sem
+    ten, vec, sca, syn = g.tensor, g.vector, g.scalar, g.sync
+    Relu, Copy = ActivationFunctionType.Relu, ActivationFunctionType.Copy
+    ADD, MULT, MAX, MIN = AluOpType.add, AluOpType.mult, AluOpType.max, AluOpType.min
+
+    def here(q):
+        return topo.host(cores[q]) == topo.host(core) and topo.chip(cores[q]) == topo.chip(core)
+
+    m = [q for q in range(N) if q != r and here(q)][0]
+    far = [q for q in range(N) if not here(q)]
+    far.sort(key=lambda q: topo.die(cores[q]) != topo.die(core))
+    a, b = far
+    far_mask = topo.mask(core, cores[a]) & topo.mask(core, cores[b])
+    near_mask = topo.mask(core, cores[m]) & ~far_mask
+    nf, nn = bin(far_mask).count("1"), bin(near_mask).count("1")
+
+    def dst(q):
+        rid, pid = topo.addr(cores[q], core)
+        return DstId(rid=rid, pnc=pid)
+
+    def blk(name, c, n=NC):
+        return T[name][:, n * c:n * c + n]
+
+    def codes(name, c):
+        return blk(name, c).bitcast(U8)
+
+    def bank(k):
+        return T["ps%d" % k][:, 0:NC]
+
+    def sem(name, c):
+        return S["%s%d" % (name, c)]
+
+    arrivals = {a: nf, b: nf, m: nn}
+
+    syn.dma_start(T.xb[:], T.x[:]).then_inc(S.lx, 16)
+    syn.dma_start(T.w1b[:], T.w1[:]).then_inc(S.l1, 16)
+    syn.dma_start(T.w2b[:], T.w2[:]).then_inc(S.l2, 16)
+    syn.wait_ge(S.xlc, 2 * nf)
+    syn.dma_start(T.w3b[:], T.w3[:]).then_inc(S.l3, 16)
+    syn.wait_ge(sem("ta", r), 4)
+    syn.dma_start(T.t[r], blk("tt", r, 512)).then_inc(S.st, 16)
+    syn.wait_ge(S.plc, 2 * nf)
+    for c in (a, b, m):
+        syn.wait_ge(sem("ta", c), 4)
+        syn.dma_start(T.t[c], blk("tt", c, 512)).then_inc(S.st, 16)
+    syn.wait_ge(sem("yc", r), 2)
+    syn.dma_start(blk("y", r, 256), blk("yt", r, 256)).then_inc(S.st, 16)
+    syn.wait_ge(S.ha, 4)
+    syn.dma_start(T.h[:], T.ht[:]).then_inc(S.st, 16)
+    for c in (m, a, b):
+        syn.wait_ge(sem("yc", c), 2)
+        syn.dma_start(blk("y", c, 256), blk("yt", c, 256)).then_inc(S.st, 16)
+    syn.wait_ge(S.st, 16 * 9)
+
+    def send_far(src, out, remote_sem, local_sem):
+        g.remote_dma_fused([RemoteDMATransfer(dst_ids=[dst(a), dst(b)], dma_engine_mask=far_mask,
+                                              remote_sem=remote_sem, srcs=[src], dsts=[out, out])],
+                           local_sem=local_sem)
+
+    def send_near(src, out, remote_sem, local_sem):
+        rid, pid = topo.addr(cores[m], core)
+        g.remote_dma(out, src, remote_sem, local_sem, pid, rid, near_mask)
+
+    g.wait_ge(S.qx, 1)
+    send_far(codes("xq", r), codes("xq", r), sem("xr", r), S.xlc)
+    send_far(blk("xs", r), blk("xs", r), sem("xr", r), S.xlc)
+    send_near(codes("xq", r), codes("xq", r), sem("xr", r), S.xlm)
+    send_near(blk("xs", r), blk("xs", r), sem("xr", r), S.xlm)
+    for c in (a, b, m):
+        g.wait_ge(sem("pc", c), 2)
+        rid, pid = topo.addr(cores[c], core)
+        g.remote_dma(T["pi%d" % r][:], T["po%d" % c][:], sem("pr", r), S.plm if c == m else S.plc, pid, rid,
+                     near_mask if c == m else far_mask)
+    g.wait_ge(S.hq, 1)
+    for ap in (codes("hq", r), blk("hs", r)):
+        g.remote_dma_fused([RemoteDMATransfer(dst_ids=[dst(a), dst(b)], dma_engine_mask=far_mask,
+                                              remote_sem=sem("hr", r), srcs=[ap], dsts=[ap, ap]),
+                            RemoteDMATransfer(dst_ids=[dst(m)], dma_engine_mask=near_mask,
+                                              remote_sem=sem("hr", r), srcs=[ap], dsts=[ap])],
+                           local_sem=S.hl)
+    g.wait_ge(S.xlm, 2 * nn)
+    g.wait_ge(S.plm, nn)
+    g.wait_ge(S.hl, 2 * (nf + nn))
+
+    def product(w, i, q, c, k, done):
+        wi = slice(NC * i, NC * i + NC)
+        ten.matmul_mx(bank(k), T[w + "q"][:, wi], T[w + "s"][:, wi], blk(q + "q", c), blk(q + "s", c),
+                      True, True).then_inc(done, 1)
+
+    def first_and_second(c, z, p, keep):
+        t = T.tt
+        lo, hi = 512 * c, 512 * c + 512
+        for i in (0, 1):
+            product("w1", i, "x", c, z[i], sem("z%d_" % i, c))
+        vec.wait_ge(sem("z0_", c), 1)
+        vec.tensor_scalar(t[:, lo:hi:4], bank(z[0]), 0.0, C1, MAX, MULT).then_inc(sem("ta", c), 1)
+        vec.tensor_scalar(t[:, lo + 1:hi:4], bank(z[0]), 0.0, -C1, MIN, MULT).then_inc(sem("ta", c), 1)
+        sca.wait_ge(sem("z1_", c), 1)
+        sca.activation(t[:, lo + 2:hi:4], bank(z[1]), Relu, scale=C1).then_inc(sem("ta", c), 1)
+        sca.activation(t[:, lo + 3:hi:4], bank(z[1]), Relu, scale=-C1).then_inc(sem("ta", c), 1)
+        vec.wait_ge(sem("ta", c), 4)
+        vec.quantize_mx(blk("tq", c), blk("ts", c), t[:, lo:hi]).then_inc(sem("tq", c), 1)
+        if c == r:
+            vec.wait_ge(S.l2, 16)
+            vec.quantize_mx(T.w2q[:], T.w2s[:], T.w2b[:]).then_inc(S.q2, 1)
+            ten.wait_ge(S.q2, 1)
+        ten.wait_ge(sem("tq", c), 1)
+        for i in (0, 1):
+            product("w2", i, "t", c, p[i], sem("p%d_" % i, c))
+        if keep:
+            return
+        po = T["po%d" % c]
+        vec.wait_ge(sem("p0_", c), 1)
+        vec.tensor_copy(po[:, 0:NC], bank(p[0])).then_inc(sem("pc", c), 1)
+        sca.wait_ge(sem("p1_", c), 1)
+        sca.activation(po[:, NC:2 * NC], bank(p[1]), Copy).then_inc(sem("pc", c), 1)
+
+    vec.wait_ge(S.lx, 16)
+    vec.quantize_mx(blk("xq", r), blk("xs", r), T.xb[:]).then_inc(S.qx, 1)
+    vec.wait_ge(S.l1, 16)
+    vec.quantize_mx(T.w1q[:], T.w1s[:], T.w1b[:]).then_inc(S.q1, 1)
+    ten.wait_ge(S.qx, 1)
+    ten.wait_ge(S.q1, 1)
+    first_and_second(r, (0, 1), (6, 7), True)
+    ten.wait_ge(sem("xr", a), 2 * arrivals[a])
+    first_and_second(a, (2, 3), (4, 5), False)
+    ten.wait_ge(sem("xr", b), 2 * arrivals[b])
+    first_and_second(b, (0, 1), (2, 3), False)
+    ten.wait_ge(sem("xr", m), 2 * arrivals[m])
+    ten.wait_ge(sem("pc", a), 2)
+    first_and_second(m, (4, 5), (0, 1), False)
+
+    vec.wait_ge(S.l3, 16)
+    vec.quantize_mx(T.w3q[:], T.w3s[:], T.w3b[:]).then_inc(S.q3, 1)
+
+    vec.wait_ge(sem("p0_", r), 1)
+    vec.wait_ge(sem("p1_", r), 1)
+    vec.wait_ge(sem("pr", a), arrivals[a])
+    pa, pm, pb = T["pi%d" % a], T["pi%d" % m], T["pi%d" % b]
+    for i in (0, 1):
+        s = slice(NC * i, NC * i + NC)
+        vec.tensor_tensor(T.acc0[:, s], bank(6 + i), pa[:, s], ADD).then_inc(S.ad0, 1)
+    vec.wait_ge(S.ad0, 2)
+    vec.wait_ge(sem("pr", m), arrivals[m])
+    vec.tensor_tensor(T.acc1[:], T.acc0[:], pm[:], ADD).then_inc(S.ad1, 1)
+    vec.wait_ge(S.ad1, 1)
+    vec.wait_ge(sem("pr", b), arrivals[b])
+    for i, done in ((0, S.ad2), (1, S.ad3)):
+        s = slice(NC * i, NC * i + NC)
+        vec.tensor_tensor(T.acc2[:, s], T.acc1[:, s], pb[:, s], ADD).then_inc(done, 1)
+    sca.wait_ge(S.ad2, 1)
+    sca.activation(T.ht[:, 0:512:4], T.acc2[:, 0:NC], Relu, scale=C2).then_inc(S.ha, 1)
+    sca.activation(T.ht[:, 1:512:4], T.acc2[:, 0:NC], Relu, scale=-C2).then_inc(S.ha, 1)
+    sca.wait_ge(S.ad3, 1)
+    sca.activation(T.ht[:, 3:512:4], T.acc2[:, NC:2 * NC], Relu, scale=-C2).then_inc(S.ha, 1)
+    vec.wait_ge(S.ad3, 1)
+    vec.tensor_scalar(T.ht[:, 2:512:4], T.acc2[:, NC:2 * NC], 0.0, C2, MAX, MULT).then_inc(S.ha, 1)
+    vec.wait_ge(S.ha, 4)
+    vec.quantize_mx(blk("hq", r), blk("hs", r), T.ht[:]).then_inc(S.hq, 1)
+
+    ten.wait_ge(S.q3, 1)
+    ten.wait_ge(S.hq, 1)
+    ten.wait_ge(sem("pc", b), 2)
+    for c, k in ((r, 2), (m, 4), (a, 0), (b, 6)):
+        if c != r:
+            ten.wait_ge(sem("hr", c), 2 * arrivals[c])
+        if c == a:
+            ten.wait_ge(sem("pc", m), 2)
+        for i in (0, 1):
+            product("w3", i, "h", c, k + i, sem("y%d_" % i, c))
+        yt = T.yt
+        vec.wait_ge(sem("y0_", c), 1)
+        vec.tensor_copy(yt[:, 256 * c:256 * c + NC], bank(k)).then_inc(sem("yc", c), 1)
+        sca.wait_ge(sem("y1_", c), 1)
+        sca.activation(yt[:, 256 * c + NC:256 * c + 256], bank(k + 1), Copy).then_inc(sem("yc", c), 1)

@@ -37,7 +37,7 @@ for _k in range(8):
     SCRATCH["ps%d" % _k] = ("psum", [128, 512], "float32")
 
 SEMAPHORES = ["lx", "l1", "l2", "l3", "qx", "q1", "q2", "q3", "ad0", "ad1", "ad2", "ad3", "ha", "hq",
-              "xlc", "xlm", "plc", "plm", "hl", "st"]
+              "xlf", "xlm", "plf", "plm", "hl", "st"]
 for _c in range(N):
     for _s in ("xr", "pr", "hr", "z0_", "z1_", "ta", "tq", "p0_", "p1_", "pc", "y0_", "y1_", "yc"):
         SEMAPHORES.append("%s%d" % (_s, _c))
@@ -63,10 +63,8 @@ def rank_program(g, core, T, topo):
     far_mask = topo.mask(core, cores[a]) & topo.mask(core, cores[b])
     near_mask = topo.mask(core, cores[m]) & ~far_mask
     nf, nn = bin(far_mask).count("1"), bin(near_mask).count("1")
-
-    def dst(q):
-        rid, pid = topo.addr(cores[q], core)
-        return DstId(rid=rid, pnc=pid)
+    engines = {a: far_mask, b: far_mask, m: near_mask}
+    arrivals = {a: nf, b: nf, m: nn}
 
     def blk(name, c, n=NC):
         return T[name][:, n * c:n * c + n]
@@ -80,16 +78,14 @@ def rank_program(g, core, T, topo):
     def sem(name, c):
         return S["%s%d" % (name, c)]
 
-    arrivals = {a: nf, b: nf, m: nn}
-
     syn.dma_start(T.xb[:], T.x[:]).then_inc(S.lx, 16)
     syn.dma_start(T.w1b[:], T.w1[:]).then_inc(S.l1, 16)
     syn.dma_start(T.w2b[:], T.w2[:]).then_inc(S.l2, 16)
-    syn.wait_ge(S.xlc, 2 * nf)
+    syn.wait_ge(S.xlf, 4 * nf)
     syn.dma_start(T.w3b[:], T.w3[:]).then_inc(S.l3, 16)
     syn.wait_ge(sem("ta", r), 4)
     syn.dma_start(T.t[r], blk("tt", r, 512)).then_inc(S.st, 16)
-    syn.wait_ge(S.plc, 2 * nf)
+    syn.wait_ge(S.plf, 2 * nf)
     for c in (a, b, m):
         syn.wait_ge(sem("ta", c), 4)
         syn.dma_start(T.t[c], blk("tt", c, 512)).then_inc(S.st, 16)
@@ -102,124 +98,141 @@ def rank_program(g, core, T, topo):
         syn.dma_start(blk("y", c, 256), blk("yt", c, 256)).then_inc(S.st, 16)
     syn.wait_ge(S.st, 16 * 9)
 
-    def send_far(src, out, remote_sem, local_sem):
-        g.remote_dma_fused([RemoteDMATransfer(dst_ids=[dst(a), dst(b)], dma_engine_mask=far_mask,
-                                              remote_sem=remote_sem, srcs=[src], dsts=[out, out])],
-                           local_sem=local_sem)
+    def send(c, ap_out, ap_in, remote_sem, local_sem):
+        rid, pid = topo.addr(cores[c], core)
+        g.remote_dma(ap_out, ap_in, remote_sem, local_sem, pid, rid, engines[c])
 
-    def send_near(src, out, remote_sem, local_sem):
-        rid, pid = topo.addr(cores[m], core)
-        g.remote_dma(out, src, remote_sem, local_sem, pid, rid, near_mask)
+    def send_two(q, ap, remote_sem, local_sem):
+        transfers = []
+        for c in (q, m):
+            rid, pid = topo.addr(cores[c], core)
+            transfers.append(RemoteDMATransfer(dst_ids=[DstId(rid=rid, pnc=pid)], dma_engine_mask=engines[c],
+                                               remote_sem=remote_sem, srcs=[ap], dsts=[ap]))
+        g.remote_dma_fused(transfers, local_sem=local_sem)
 
+    x_out = (codes("xq", r), blk("xs", r))
+    h_out = (codes("hq", r), blk("hs", r))
     g.wait_ge(S.qx, 1)
-    send_far(codes("xq", r), codes("xq", r), sem("xr", r), S.xlc)
-    send_far(blk("xs", r), blk("xs", r), sem("xr", r), S.xlc)
-    send_near(codes("xq", r), codes("xq", r), sem("xr", r), S.xlm)
-    send_near(blk("xs", r), blk("xs", r), sem("xr", r), S.xlm)
+    for c in (a, b, m):
+        for ap in x_out:
+            send(c, ap, ap, sem("xr", r), S.xlm if c == m else S.xlf)
     for c in (a, b, m):
         g.wait_ge(sem("pc", c), 2)
-        rid, pid = topo.addr(cores[c], core)
-        g.remote_dma(T["pi%d" % r][:], T["po%d" % c][:], sem("pr", r), S.plm if c == m else S.plc, pid, rid,
-                     near_mask if c == m else far_mask)
+        send(c, T["pi%d" % r][:], T["po%d" % c][:], sem("pr", r), S.plm if c == m else S.plf)
     g.wait_ge(S.hq, 1)
-    for ap in (codes("hq", r), blk("hs", r)):
-        g.remote_dma_fused([RemoteDMATransfer(dst_ids=[dst(a), dst(b)], dma_engine_mask=far_mask,
-                                              remote_sem=sem("hr", r), srcs=[ap], dsts=[ap, ap]),
-                            RemoteDMATransfer(dst_ids=[dst(m)], dma_engine_mask=near_mask,
-                                              remote_sem=sem("hr", r), srcs=[ap], dsts=[ap])],
-                           local_sem=S.hl)
+    for ap in h_out:
+        send_two(a, ap, sem("hr", r), S.hl)
+    for ap in h_out:
+        send(b, ap, ap, sem("hr", r), S.hl)
     g.wait_ge(S.xlm, 2 * nn)
     g.wait_ge(S.plm, nn)
-    g.wait_ge(S.hl, 2 * (nf + nn))
+    g.wait_ge(S.hl, 4 * nf + 2 * nn)
 
     def product(w, i, q, c, k, done):
         wi = slice(NC * i, NC * i + NC)
         ten.matmul_mx(bank(k), T[w + "q"][:, wi], T[w + "s"][:, wi], blk(q + "q", c), blk(q + "s", c),
                       True, True).then_inc(done, 1)
 
-    def first_and_second(c, z, p, keep):
-        t = T.tt
-        lo, hi = 512 * c, 512 * c + 512
+    def first(c, k):
         for i in (0, 1):
-            product("w1", i, "x", c, z[i], sem("z%d_" % i, c))
+            product("w1", i, "x", c, k + i, sem("z%d_" % i, c))
+
+    def make(c, k):
+        t, lo, hi = T.tt, 512 * c, 512 * c + 512
         vec.wait_ge(sem("z0_", c), 1)
-        vec.tensor_scalar(t[:, lo:hi:4], bank(z[0]), 0.0, C1, MAX, MULT).then_inc(sem("ta", c), 1)
-        vec.tensor_scalar(t[:, lo + 1:hi:4], bank(z[0]), 0.0, -C1, MIN, MULT).then_inc(sem("ta", c), 1)
+        vec.tensor_scalar(t[:, lo:hi:4], bank(k), 0.0, C1, MAX, MULT).then_inc(sem("ta", c), 1)
+        vec.tensor_scalar(t[:, lo + 1:hi:4], bank(k), 0.0, -C1, MIN, MULT).then_inc(sem("ta", c), 1)
         sca.wait_ge(sem("z1_", c), 1)
-        sca.activation(t[:, lo + 2:hi:4], bank(z[1]), Relu, scale=C1).then_inc(sem("ta", c), 1)
-        sca.activation(t[:, lo + 3:hi:4], bank(z[1]), Relu, scale=-C1).then_inc(sem("ta", c), 1)
+        sca.activation(t[:, lo + 2:hi:4], bank(k + 1), Relu, scale=C1).then_inc(sem("ta", c), 1)
+        sca.activation(t[:, lo + 3:hi:4], bank(k + 1), Relu, scale=-C1).then_inc(sem("ta", c), 1)
+
+    def pack(c):
         vec.wait_ge(sem("ta", c), 4)
-        vec.quantize_mx(blk("tq", c), blk("ts", c), t[:, lo:hi]).then_inc(sem("tq", c), 1)
-        if c == r:
-            vec.wait_ge(S.l2, 16)
-            vec.quantize_mx(T.w2q[:], T.w2s[:], T.w2b[:]).then_inc(S.q2, 1)
-            ten.wait_ge(S.q2, 1)
+        vec.quantize_mx(blk("tq", c), blk("ts", c), blk("tt", c, 512)).then_inc(sem("tq", c), 1)
+
+    def second(c, k):
         ten.wait_ge(sem("tq", c), 1)
         for i in (0, 1):
-            product("w2", i, "t", c, p[i], sem("p%d_" % i, c))
-        if keep:
-            return
+            product("w2", i, "t", c, k + i, sem("p%d_" % i, c))
+
+    def lift(c, k):
         po = T["po%d" % c]
         vec.wait_ge(sem("p0_", c), 1)
-        vec.tensor_copy(po[:, 0:NC], bank(p[0])).then_inc(sem("pc", c), 1)
+        vec.tensor_copy(po[:, 0:NC], bank(k)).then_inc(sem("pc", c), 1)
         sca.wait_ge(sem("p1_", c), 1)
-        sca.activation(po[:, NC:2 * NC], bank(p[1]), Copy).then_inc(sem("pc", c), 1)
+        sca.activation(po[:, NC:2 * NC], bank(k + 1), Copy).then_inc(sem("pc", c), 1)
+
+    ten.wait_ge(S.qx, 1)
+    ten.wait_ge(S.q1, 1)
+    first(r, 0)
+    ten.wait_ge(S.q2, 1)
+    second(r, 6)
+    ten.wait_ge(sem("xr", a), 2 * arrivals[a])
+    first(a, 2)
+    second(a, 4)
+    ten.wait_ge(sem("xr", b), 2 * arrivals[b])
+    first(b, 0)
+    ten.wait_ge(sem("xr", m), 2 * arrivals[m])
+    first(m, 2)
+    ten.wait_ge(sem("pc", a), 2)
+    second(b, 4)
+    second(m, 0)
 
     vec.wait_ge(S.lx, 16)
     vec.quantize_mx(blk("xq", r), blk("xs", r), T.xb[:]).then_inc(S.qx, 1)
     vec.wait_ge(S.l1, 16)
     vec.quantize_mx(T.w1q[:], T.w1s[:], T.w1b[:]).then_inc(S.q1, 1)
-    ten.wait_ge(S.qx, 1)
-    ten.wait_ge(S.q1, 1)
-    first_and_second(r, (0, 1), (6, 7), True)
-    ten.wait_ge(sem("xr", a), 2 * arrivals[a])
-    first_and_second(a, (2, 3), (4, 5), False)
-    ten.wait_ge(sem("xr", b), 2 * arrivals[b])
-    first_and_second(b, (0, 1), (2, 3), False)
-    ten.wait_ge(sem("xr", m), 2 * arrivals[m])
-    ten.wait_ge(sem("pc", a), 2)
-    first_and_second(m, (4, 5), (0, 1), False)
+    make(r, 0)
+    pack(r)
+    vec.wait_ge(S.l2, 16)
+    vec.quantize_mx(T.w2q[:], T.w2s[:], T.w2b[:]).then_inc(S.q2, 1)
+    make(a, 2)
+    pack(a)
+    lift(a, 4)
+    make(b, 0)
+    pack(b)
+    make(m, 2)
+    lift(b, 4)
+    pack(m)
+    lift(m, 0)
 
-    vec.wait_ge(S.l3, 16)
-    vec.quantize_mx(T.w3q[:], T.w3s[:], T.w3b[:]).then_inc(S.q3, 1)
-
+    pa, pm, pb = T["pi%d" % a], T["pi%d" % m], T["pi%d" % b]
+    halves = (slice(0, NC), slice(NC, 2 * NC))
     vec.wait_ge(sem("p0_", r), 1)
     vec.wait_ge(sem("p1_", r), 1)
     vec.wait_ge(sem("pr", a), arrivals[a])
-    pa, pm, pb = T["pi%d" % a], T["pi%d" % m], T["pi%d" % b]
     for i in (0, 1):
-        s = slice(NC * i, NC * i + NC)
-        vec.tensor_tensor(T.acc0[:, s], bank(6 + i), pa[:, s], ADD).then_inc(S.ad0, 1)
+        vec.tensor_tensor(T.acc0[:, halves[i]], bank(6 + i), pa[:, halves[i]], ADD).then_inc(S.ad0, 1)
     vec.wait_ge(S.ad0, 2)
     vec.wait_ge(sem("pr", m), arrivals[m])
     vec.tensor_tensor(T.acc1[:], T.acc0[:], pm[:], ADD).then_inc(S.ad1, 1)
     vec.wait_ge(S.ad1, 1)
     vec.wait_ge(sem("pr", b), arrivals[b])
     for i, done in ((0, S.ad2), (1, S.ad3)):
-        s = slice(NC * i, NC * i + NC)
-        vec.tensor_tensor(T.acc2[:, s], T.acc1[:, s], pb[:, s], ADD).then_inc(done, 1)
+        vec.tensor_tensor(T.acc2[:, halves[i]], T.acc1[:, halves[i]], pb[:, halves[i]], ADD).then_inc(done, 1)
     sca.wait_ge(S.ad2, 1)
-    sca.activation(T.ht[:, 0:512:4], T.acc2[:, 0:NC], Relu, scale=C2).then_inc(S.ha, 1)
-    sca.activation(T.ht[:, 1:512:4], T.acc2[:, 0:NC], Relu, scale=-C2).then_inc(S.ha, 1)
+    sca.activation(T.ht[:, 0:512:4], T.acc2[:, halves[0]], Relu, scale=C2).then_inc(S.ha, 1)
+    sca.activation(T.ht[:, 1:512:4], T.acc2[:, halves[0]], Relu, scale=-C2).then_inc(S.ha, 1)
     sca.wait_ge(S.ad3, 1)
-    sca.activation(T.ht[:, 3:512:4], T.acc2[:, NC:2 * NC], Relu, scale=-C2).then_inc(S.ha, 1)
+    sca.activation(T.ht[:, 3:512:4], T.acc2[:, halves[1]], Relu, scale=-C2).then_inc(S.ha, 1)
     vec.wait_ge(S.ad3, 1)
-    vec.tensor_scalar(T.ht[:, 2:512:4], T.acc2[:, NC:2 * NC], 0.0, C2, MAX, MULT).then_inc(S.ha, 1)
+    vec.tensor_scalar(T.ht[:, 2:512:4], T.acc2[:, halves[1]], 0.0, C2, MAX, MULT).then_inc(S.ha, 1)
     vec.wait_ge(S.ha, 4)
     vec.quantize_mx(blk("hq", r), blk("hs", r), T.ht[:]).then_inc(S.hq, 1)
+    vec.wait_ge(S.l3, 16)
+    vec.quantize_mx(T.w3q[:], T.w3s[:], T.w3b[:]).then_inc(S.q3, 1)
 
-    ten.wait_ge(S.q3, 1)
     ten.wait_ge(S.hq, 1)
-    ten.wait_ge(sem("pc", b), 2)
-    for c, k in ((r, 2), (m, 4), (a, 0), (b, 6)):
+    ten.wait_ge(S.q3, 1)
+    for c, k, freed in ((r, 2, None), (m, 4, b), (a, 0, m), (b, 6, None)):
         if c != r:
             ten.wait_ge(sem("hr", c), 2 * arrivals[c])
-        if c == a:
-            ten.wait_ge(sem("pc", m), 2)
+        if freed is not None:
+            ten.wait_ge(sem("pc", freed), 2)
         for i in (0, 1):
             product("w3", i, "h", c, k + i, sem("y%d_" % i, c))
-        yt = T.yt
+        lo = 256 * c
         vec.wait_ge(sem("y0_", c), 1)
-        vec.tensor_copy(yt[:, 256 * c:256 * c + NC], bank(k)).then_inc(sem("yc", c), 1)
+        vec.tensor_copy(T.yt[:, lo:lo + NC], bank(k)).then_inc(sem("yc", c), 1)
         sca.wait_ge(sem("y1_", c), 1)
-        sca.activation(yt[:, 256 * c + NC:256 * c + 256], bank(k + 1), Copy).then_inc(sem("yc", c), 1)
+        sca.activation(T.yt[:, lo + NC:lo + 256], bank(k + 1), Copy).then_inc(sem("yc", c), 1)

from concourse.bass import DstId, RemoteDMATransfer
from concourse.mybir import dt, AluOpType, ActivationFunctionType

N = 4
NC = 128
C1, C2 = 0.031, 0.0155
U8 = dt.uint8

SCRATCH = {
    "xb": ("sbuf", [128, 512], "bfloat16"),
    "w1b": ("sbuf", [128, 1024], "bfloat16"),
    "w2b": ("sbuf", [128, 1024], "bfloat16"),
    "w3b": ("sbuf", [128, 1024], "bfloat16"),
    "xq": ("sbuf", [128, N * NC], "float8_e4m3fn_x4"),
    "xs": ("sbuf", [128, N * NC], "uint8"),
    "w1q": ("sbuf", [128, 256], "float8_e4m3fn_x4"),
    "w1s": ("sbuf", [128, 256], "uint8"),
    "w2q": ("sbuf", [128, 256], "float8_e4m3fn_x4"),
    "w2s": ("sbuf", [128, 256], "uint8"),
    "w3q": ("sbuf", [128, 256], "float8_e4m3fn_x4"),
    "w3s": ("sbuf", [128, 256], "uint8"),
    "tq": ("sbuf", [128, N * NC], "float8_e4m3fn_x4"),
    "ts": ("sbuf", [128, N * NC], "uint8"),
    "hq": ("sbuf", [128, N * NC], "float8_e4m3fn_x4"),
    "hs": ("sbuf", [128, N * NC], "uint8"),
    "tt": ("sbuf", [128, N * 512], "bfloat16"),
    "ht": ("sbuf", [128, 512], "bfloat16"),
    "acc0": ("sbuf", [128, 256], "float32"),
    "acc1": ("sbuf", [128, 256], "float32"),
    "acc2": ("sbuf", [128, 256], "float32"),
    "yt": ("sbuf", [128, N * 256], "float32"),
}
for _c in range(N):
    SCRATCH["po%d" % _c] = ("sbuf", [128, 256], "float32")
    SCRATCH["pi%d" % _c] = ("sbuf", [128, 256], "float32")
for _k in range(8):
    SCRATCH["ps%d" % _k] = ("psum", [128, 512], "float32")

SEMAPHORES = ["lx", "l1", "l2", "l3", "qx", "q1", "q2", "q3", "ad0", "ad1", "ad2", "ad3", "ha", "hq",
              "xlf", "xlm", "plf", "plm", "hl", "st"]
for _c in range(N):
    for _s in ("xr", "pr", "hr", "z0_", "z1_", "ta", "tq", "p0_", "p1_", "pc", "y0_", "y1_", "yc"):
        SEMAPHORES.append("%s%d" % (_s, _c))


def rank_program(g, core, T, topo):
    r = T.rank_of(core)
    if r is None:
        return
    cores = T.cores
    S = T.sem
    ten, vec, sca, syn = g.tensor, g.vector, g.scalar, g.sync
    Relu, Copy = ActivationFunctionType.Relu, ActivationFunctionType.Copy
    ADD, MULT, MAX, MIN = AluOpType.add, AluOpType.mult, AluOpType.max, AluOpType.min

    def here(q):
        return topo.host(cores[q]) == topo.host(core) and topo.chip(cores[q]) == topo.chip(core)

    m = [q for q in range(N) if q != r and here(q)][0]
    far = [q for q in range(N) if not here(q)]
    far.sort(key=lambda q: topo.die(cores[q]) != topo.die(core))
    a, b = far
    far_mask = topo.mask(core, cores[a]) & topo.mask(core, cores[b])
    near_mask = topo.mask(core, cores[m]) & ~far_mask
    nf, nn = bin(far_mask).count("1"), bin(near_mask).count("1")
    engines = {a: far_mask, b: far_mask, m: near_mask}
    arrivals = {a: nf, b: nf, m: nn}

    def blk(name, c, n=NC):
        return T[name][:, n * c:n * c + n]

    def codes(name, c):
        return blk(name, c).bitcast(U8)

    def bank(k):
        return T["ps%d" % k][:, 0:NC]

    def sem(name, c):
        return S["%s%d" % (name, c)]

    syn.dma_start(T.xb[:], T.x[:]).then_inc(S.lx, 16)
    syn.dma_start(T.w1b[:], T.w1[:]).then_inc(S.l1, 16)
    syn.dma_start(T.w2b[:], T.w2[:]).then_inc(S.l2, 16)
    syn.wait_ge(S.xlf, 4 * nf)
    syn.dma_start(T.w3b[:], T.w3[:]).then_inc(S.l3, 16)
    syn.wait_ge(sem("ta", r), 4)
    syn.dma_start(T.t[r], blk("tt", r, 512)).then_inc(S.st, 16)
    syn.wait_ge(S.plf, 2 * nf)
    for c in (a, b, m):
        syn.wait_ge(sem("ta", c), 4)
        syn.dma_start(T.t[c], blk("tt", c, 512)).then_inc(S.st, 16)
    syn.wait_ge(sem("yc", r), 2)
    syn.dma_start(blk("y", r, 256), blk("yt", r, 256)).then_inc(S.st, 16)
    syn.wait_ge(S.ha, 4)
    syn.dma_start(T.h[:], T.ht[:]).then_inc(S.st, 16)
    for c in (m, a, b):
        syn.wait_ge(sem("yc", c), 2)
        syn.dma_start(blk("y", c, 256), blk("yt", c, 256)).then_inc(S.st, 16)
    syn.wait_ge(S.st, 16 * 9)

    def send(c, ap_out, ap_in, remote_sem, local_sem):
        rid, pid = topo.addr(cores[c], core)
        g.remote_dma(ap_out, ap_in, remote_sem, local_sem, pid, rid, engines[c])

    def send_two(q, ap, remote_sem, local_sem):
        transfers = []
        for c in (q, m):
            rid, pid = topo.addr(cores[c], core)
            transfers.append(RemoteDMATransfer(dst_ids=[DstId(rid=rid, pnc=pid)], dma_engine_mask=engines[c],
                                               remote_sem=remote_sem, srcs=[ap], dsts=[ap]))
        g.remote_dma_fused(transfers, local_sem=local_sem)

    x_out = (codes("xq", r), blk("xs", r))
    h_out = (codes("hq", r), blk("hs", r))
    g.wait_ge(S.qx, 1)
    for c in (a, b, m):
        for ap in x_out:
            send(c, ap, ap, sem("xr", r), S.xlm if c == m else S.xlf)
    for c in (a, b, m):
        g.wait_ge(sem("pc", c), 2)
        send(c, T["pi%d" % r][:], T["po%d" % c][:], sem("pr", r), S.plm if c == m else S.plf)
    g.wait_ge(S.hq, 1)
    for ap in h_out:
        send_two(a, ap, sem("hr", r), S.hl)
    for ap in h_out:
        send(b, ap, ap, sem("hr", r), S.hl)
    g.wait_ge(S.xlm, 2 * nn)
    g.wait_ge(S.plm, nn)
    g.wait_ge(S.hl, 4 * nf + 2 * nn)

    def product(w, i, q, c, k, done):
        wi = slice(NC * i, NC * i + NC)
        ten.matmul_mx(bank(k), T[w + "q"][:, wi], T[w + "s"][:, wi], blk(q + "q", c), blk(q + "s", c),
                      True, True).then_inc(done, 1)

    def first(c, k):
        for i in (0, 1):
            product("w1", i, "x", c, k + i, sem("z%d_" % i, c))

    def make(c, k):
        t, lo, hi = T.tt, 512 * c, 512 * c + 512
        vec.wait_ge(sem("z0_", c), 1)
        vec.tensor_scalar(t[:, lo:hi:4], bank(k), 0.0, C1, MAX, MULT).then_inc(sem("ta", c), 1)
        vec.tensor_scalar(t[:, lo + 1:hi:4], bank(k), 0.0, -C1, MIN, MULT).then_inc(sem("ta", c), 1)
        sca.wait_ge(sem("z1_", c), 1)
        sca.activation(t[:, lo + 2:hi:4], bank(k + 1), Relu, scale=C1).then_inc(sem("ta", c), 1)
        sca.activation(t[:, lo + 3:hi:4], bank(k + 1), Relu, scale=-C1).then_inc(sem("ta", c), 1)

    def pack(c):
        vec.wait_ge(sem("ta", c), 4)
        vec.quantize_mx(blk("tq", c), blk("ts", c), blk("tt", c, 512)).then_inc(sem("tq", c), 1)

    def second(c, k):
        ten.wait_ge(sem("tq", c), 1)
        for i in (0, 1):
            product("w2", i, "t", c, k + i, sem("p%d_" % i, c))

    def lift(c, k):
        po = T["po%d" % c]
        vec.wait_ge(sem("p0_", c), 1)
        vec.tensor_copy(po[:, 0:NC], bank(k)).then_inc(sem("pc", c), 1)
        sca.wait_ge(sem("p1_", c), 1)
        sca.activation(po[:, NC:2 * NC], bank(k + 1), Copy).then_inc(sem("pc", c), 1)

    ten.wait_ge(S.qx, 1)
    ten.wait_ge(S.q1, 1)
    first(r, 0)
    ten.wait_ge(S.q2, 1)
    second(r, 6)
    ten.wait_ge(sem("xr", a), 2 * arrivals[a])
    first(a, 2)
    second(a, 4)
    ten.wait_ge(sem("xr", b), 2 * arrivals[b])
    first(b, 0)
    ten.wait_ge(sem("xr", m), 2 * arrivals[m])
    first(m, 2)
    ten.wait_ge(sem("pc", a), 2)
    second(b, 4)
    second(m, 0)

    vec.wait_ge(S.lx, 16)
    vec.quantize_mx(blk("xq", r), blk("xs", r), T.xb[:]).then_inc(S.qx, 1)
    vec.wait_ge(S.l1, 16)
    vec.quantize_mx(T.w1q[:], T.w1s[:], T.w1b[:]).then_inc(S.q1, 1)
    make(r, 0)
    pack(r)
    vec.wait_ge(S.l2, 16)
    vec.quantize_mx(T.w2q[:], T.w2s[:], T.w2b[:]).then_inc(S.q2, 1)
    make(a, 2)
    pack(a)
    lift(a, 4)
    make(b, 0)
    pack(b)
    make(m, 2)
    lift(b, 4)
    pack(m)
    lift(m, 0)

    pa, pm, pb = T["pi%d" % a], T["pi%d" % m], T["pi%d" % b]
    halves = (slice(0, NC), slice(NC, 2 * NC))
    vec.wait_ge(sem("p0_", r), 1)
    vec.wait_ge(sem("p1_", r), 1)
    vec.wait_ge(sem("pr", a), arrivals[a])
    for i in (0, 1):
        vec.tensor_tensor(T.acc0[:, halves[i]], bank(6 + i), pa[:, halves[i]], ADD).then_inc(S.ad0, 1)
    vec.wait_ge(S.ad0, 2)
    vec.wait_ge(sem("pr", m), arrivals[m])
    vec.tensor_tensor(T.acc1[:], T.acc0[:], pm[:], ADD).then_inc(S.ad1, 1)
    vec.wait_ge(S.ad1, 1)
    vec.wait_ge(sem("pr", b), arrivals[b])
    for i, done in ((0, S.ad2), (1, S.ad3)):
        vec.tensor_tensor(T.acc2[:, halves[i]], T.acc1[:, halves[i]], pb[:, halves[i]], ADD).then_inc(done, 1)
    sca.wait_ge(S.ad2, 1)
    sca.activation(T.ht[:, 0:512:4], T.acc2[:, halves[0]], Relu, scale=C2).then_inc(S.ha, 1)
    sca.activation(T.ht[:, 1:512:4], T.acc2[:, halves[0]], Relu, scale=-C2).then_inc(S.ha, 1)
    sca.wait_ge(S.ad3, 1)
    sca.activation(T.ht[:, 3:512:4], T.acc2[:, halves[1]], Relu, scale=-C2).then_inc(S.ha, 1)
    vec.wait_ge(S.ad3, 1)
    vec.tensor_scalar(T.ht[:, 2:512:4], T.acc2[:, halves[1]], 0.0, C2, MAX, MULT).then_inc(S.ha, 1)
    vec.wait_ge(S.ha, 4)
    vec.quantize_mx(blk("hq", r), blk("hs", r), T.ht[:]).then_inc(S.hq, 1)
    vec.wait_ge(S.l3, 16)
    vec.quantize_mx(T.w3q[:], T.w3s[:], T.w3b[:]).then_inc(S.q3, 1)

    ten.wait_ge(S.hq, 1)
    ten.wait_ge(S.q3, 1)
    for c, k, freed in ((r, 2, None), (m, 4, b), (a, 0, m), (b, 6, None)):
        if c != r:
            ten.wait_ge(sem("hr", c), 2 * arrivals[c])
        if freed is not None:
            ten.wait_ge(sem("pc", freed), 2)
        for i in (0, 1):
            product("w3", i, "h", c, k + i, sem("y%d_" % i, c))
        lo = 256 * c
        vec.wait_ge(sem("y0_", c), 1)
        vec.tensor_copy(T.yt[:, lo:lo + NC], bank(k)).then_inc(sem("yc", c), 1)
        sca.wait_ge(sem("y1_", c), 1)
        sca.activation(T.yt[:, lo + NC:lo + 256], bank(k + 1), Copy).then_inc(sem("yc", c), 1)
